import numpy as np
import ml_dtypes


def mxq(x, axis, fmt="e4m3"):
    dtype, down = {"e4m3": (ml_dtypes.float8_e4m3fn, 7), "e5m2": (ml_dtypes.float8_e5m2, 14)}[fmt]
    v = np.moveaxis(np.asarray(x, np.float32).astype(ml_dtypes.bfloat16).astype(np.float64), axis, -1)
    blocks = v.reshape(v.shape[:-1] + (-1, 32))
    amax = np.abs(blocks).max(-1, keepdims=True)
    byte = np.maximum(np.where(amax > 0, np.frexp(amax)[1] - 1 + 127, 0) - down, 1)
    scale = np.exp2(byte - 127.0)
    codes = (blocks / scale).astype(np.float32).astype(dtype).astype(np.float64)
    return np.moveaxis((codes * scale).reshape(v.shape), -1, axis)


WIDE = False


def mx_kscale(k):
    if not WIDE:
        return np.ones(k)
    levels = np.array([10, -10, 5, -5, 0])
    if k % 512:
        return np.exp2(np.random.permutation(np.resize(levels, k // 32))).repeat(32)
    a = np.empty((k // 512, 16))
    for p in range(k // 512):
        a[p, :8] = np.random.permutation(np.resize(levels, 8))
        for g in range(8):
            far = levels[np.abs(levels - a[p, g]) >= 10]
            a[p, g + 8] = far[np.random.randint(len(far))]
    return np.exp2(a.ravel()).repeat(32)


def f64(x):
    return np.asarray(x).astype(np.float64)


def striped(idx):
    return np.tile(idx.reshape(-1, 16).T, (8, 1)).astype(np.uint16)


def unstriped(offs):
    return offs[:16].T.reshape(-1).astype(np.int64)


E2M1 = np.array([0.0, 0.5, 1.0, 1.5, 2.0, 3.0, 4.0, 6.0, -0.0, -0.5, -1.0, -1.5, -2.0, -3.0, -4.0, -6.0])


def pack_weight(w, fmt):
    k, n = w.shape
    w = f64(np.asarray(w, np.float32).astype(ml_dtypes.bfloat16)).reshape(k // 32, 32, n)
    amax = np.abs(w).max(1)
    if fmt == "e4m3":
        byte = np.frexp(amax)[1] - 1 + 127 - 7
    else:
        mant, ex = np.frexp(amax / 6.0)
        byte = np.where(mant > 0.5, ex, ex - 1) + 127
    byte = np.clip(np.where(amax > 0, byte, 1), 1, 254)
    scaled = (w * np.exp2(127.0 - byte)[:, None, :]).reshape(k, n).astype(np.float32)
    by_word = np.ascontiguousarray(scaled.reshape(k // 512, 128, 4, n).transpose(0, 1, 3, 2))
    if fmt == "e4m3":
        words = by_word.astype(ml_dtypes.float8_e4m3fn).view(np.uint8)
    else:
        c = by_word.astype(ml_dtypes.float4_e2m1fn).view(np.uint8) & 0xF
        words = (c[..., 0::2] | (c[..., 1::2] << 4)).reshape(k // 512, 128, 2 * n)
    return np.ascontiguousarray(words), np.ascontiguousarray(byte.astype(np.uint8).reshape(k // 512, 16, n))


def unpack_weight(words, scales, fmt):
    g, _, n = scales.shape
    words = np.ascontiguousarray(words).reshape(g, 128, n, -1)
    if fmt == "e4m3":
        vals = words.view(ml_dtypes.float8_e4m3fn).astype(np.float64)
    else:
        nib = np.empty((g, 128, n, 4), np.uint8)
        nib[..., 0::2] = words & 0xF
        nib[..., 1::2] = words >> 4
        vals = E2M1[nib]
    vals = vals * np.repeat(np.exp2(scales.astype(np.float64) - 127.0), 8, axis=1)[..., None]
    return vals.transpose(0, 1, 3, 2).reshape(g * 512, n)


def gelu(v):
    return 0.5 * v * (1.0 + np.tanh(np.sqrt(2.0 / np.pi) * (v + 0.044715 * v**3)))


def bf(x):
    return np.asarray(x, np.float32).astype(ml_dtypes.bfloat16)


def planes(Y):
    n, m = Y.shape
    b = f64(bf(Y)).reshape(n // 32, 32, m)
    amax = np.abs(b).max(1)
    byte = np.clip(np.where(amax > 0, np.frexp(amax)[1] - 1 + 127 - 7, 1), 1, 254)
    codes = (b * np.exp2(127.0 - byte)[:, None, :]).reshape(n, m).astype(np.float32).astype(ml_dtypes.float8_e4m3fn).view(np.uint8)
    words = codes.reshape(n // 512, 128, 4, m).transpose(0, 1, 3, 2)
    return np.ascontiguousarray(words), np.ascontiguousarray(byte.astype(np.uint8).reshape(n // 512, 16, m))


K, T, S, H, N, T2, P = 1024, 4096, 1024, 512, 384, 2048, 1024

def setup_inputs():
    n = np.random.standard_normal
    s = mx_kscale(K)[:, None]
    u = mx_kscale(H)[:, None]
    d = {}
    d["tab_words"], d["tab_scales"] = pack_weight(n((K, T)) * s, "e4m3")
    d["offs"] = striped(np.random.permutation(T)[:S])
    d["w1"] = (n((K, H)) / s / K ** 0.5).astype(np.float32)
    d["w2"] = (n((K, H)) / s / K ** 0.5).astype(np.float32)
    d["w3_words"], d["w3_scales"] = pack_weight(n((K, H)) / s / K ** 0.5, "e2m1")
    d["gain"] = (np.exp(0.3 * n(H)) * u[:, 0]).astype(np.float32)
    d["wgs"] = np.exp(0.3 * n((128, S))).astype(np.float32)
    d["page0"] = (n((H, T2)) * u).astype(np.float32)
    d["offs2"] = striped(np.random.permutation(T2)[:S])
    d["offs3"] = striped(np.random.permutation(T2)[:P])
    d["w4_words"], d["w4_scales"] = pack_weight(n((H, N)) / u / H ** 0.5, "e4m3")
    d["mnt"] = n((N, P)).astype(np.float32)
    return d

def reference(tab_words, tab_scales, offs, w1, w2, w3_words, w3_scales, gain, wgs, page0,
              offs2, offs3, w4_words, w4_scales, mnt):
    v = unpack_weight(tab_words, tab_scales, "e4m3")[:, unstriped(offs)]
    a = mxq(f64(w1), 0, "e4m3").T @ v
    b = mxq(f64(w2), 0, "e4m3").T @ v
    c = unpack_weight(w3_words, w3_scales, "e2m1").T @ v
    h = f64(gain)[:, None] * (np.maximum(a, b) - c)
    page = f64(page0).copy()
    page[:, unstriped(offs2)] = np.tile(f64(wgs), (H // 128, 1)) * h
    x = np.abs(page[:, unstriped(offs3)])
    y = (unpack_weight(w4_words, w4_scales, "e4m3").T @ mxq(x, 0, "e4m3")) + f64(mnt)
    words, scales = planes(page)
    return y, page, words, scales

@@ -1,0 +1,281 @@
+from contextlib import ExitStack
+
+import concourse.mybir as mybir
+from concourse.masks import make_identity
+
+K, T, S, H, N, T2, M = 1024, 4096, 1024, 512, 384, 2048, 1024
+FLOPS = 3 * 2 * K * H * S + 2 * H * N * M
+
+F32 = mybir.dt.float32
+BF16 = mybir.dt.bfloat16
+I32 = mybir.dt.int32
+U32 = mybir.dt.uint32
+U16 = mybir.dt.uint16
+U8 = mybir.dt.uint8
+FP8X4 = mybir.dt.float8_e4m3fn_x4
+FP4X4 = mybir.dt.float4_e2m1fn_x4
+ACT = mybir.ActivationFunctionType
+ALU = mybir.AluOpType
+
+P = 128
+PACK = 4
+PASSES = K // (P * PACK)
+BANK = 512
+JB = S // P
+CHUNKS = T2 // BANK
+
+
+def tile_list_chord_span_archive_kernel(
+    tc, tab_words, tab_scales, offs, w1, w2, w3_words, w3_scales, gain, wgs, page0,
+    offs2, offs3, w4_words, w4_scales, mnt, out_0, out_1, out_2, out_3,
+):
+    nc = tc.nc
+    with ExitStack() as ctx:
+        lists = ctx.enter_context(tc.tile_pool(name="lists", bufs=1))
+        keep = ctx.enter_context(tc.tile_pool(name="keep", bufs=1))
+        ring = ctx.enter_context(tc.tile_pool(name="ring", bufs=1))
+        psum = ctx.enter_context(tc.psum_pool(name="psum", bufs=1))
+
+        idx1 = lists.tile([P, S // 16], U16, name="idx1")
+        idx2 = lists.tile([P, S // 16], U16, name="idx2")
+        idx3 = lists.tile([P, M // 16], U16, name="idx3")
+
+        tab_sc = keep.tile([P, PASSES, T], U8, name="tab_sc", align_bytes=64)
+        w3_sc = keep.tile([P, PASSES, H], U8, name="w3_sc", align_bytes=64)
+        w4_sc = keep.tile([P, N], U8, name="w4_sc", align_bytes=64)
+        nc.vector.memset(tab_sc[:, 0, :].bitcast(I32), 0)
+        nc.gpsimd.memset(tab_sc[:, 1, :].bitcast(I32), 0)
+        nc.vector.memset(w3_sc[:].bitcast(I32), 0)
+        nc.vector.memset(w4_sc[:].bitcast(I32), 0)
+
+        nc.sync.dma_start(idx1[:], offs)
+        tab_w = []
+        for a in range(PASSES):
+            tw = keep.tile([P, T], U32, name=f"tab_w{a}")
+            nc.sync.dma_start(
+                tw[:].bitcast(I32), tab_words[a].rearrange("p t i -> p (t i)").bitcast(I32)
+            )
+            tab_w.append(tw)
+            if a == 0:
+                for q in range(4):
+                    nc.sync.dma_start(
+                        tab_sc[32 * q : 32 * q + 4, :, :].bitcast(I32),
+                        tab_scales[:, 4 * q : 4 * q + 4, :].rearrange("a r c -> r a c").bitcast(I32),
+                    )
+        w3_w = keep.tile([P, PASSES, 2 * H], U8, name="w3_w", align_bytes=64)
+        nc.sync.dma_start(w3_w[:].bitcast(I32), w3_words.rearrange("a p c -> p a c").bitcast(I32))
+        for q in range(4):
+            nc.sync.dma_start(
+                w3_sc[32 * q : 32 * q + 4, :, :].bitcast(I32),
+                w3_scales[:, 4 * q : 4 * q + 4, :].rearrange("a r c -> r a c").bitcast(I32),
+            )
+
+        pieces = [(0, 0, 0, H), (0, 1, 0, H), (1, 0, 0, H), (1, 1, 0, H // 2), (1, 1, H // 2, H // 2)]
+        raws = []
+        for wi, a, c0, cn in pieces:
+            raw = ring.tile([P, PACK, cn], F32, name="raw", tag="raw" if cn == H else "rawh", bufs=3 if cn == H else 2)
+            rows = (w1, w2)[wi][a * 512 : (a + 1) * 512, c0 : c0 + cn]
+            nc.sync.dma_start(raw[:], rows.rearrange("(p j) c -> p j c", j=PACK))
+            raws.append(raw)
+
+        gain_sb = keep.tile([P, PACK], F32, name="gain_sb")
+        nc.sync.dma_start(gain_sb[:], gain.rearrange("(p t) -> p t", t=PACK))
+        nc.sync.dma_start(idx2[:], offs2)
+        wgs_q = wgs.rearrange("(q t) j -> q t j", t=PACK)
+        page0_t = page0.rearrange("(p t) m -> t p m", t=PACK)
+        out1_t = out_1.rearrange("(p t) m -> t p m", t=PACK)
+        wg = [None] * PACK
+        page = []
+        for t in range(PACK):
+            if t != 3:
+                nt = 2 if t == 2 else 1
+                wt = keep.tile([P, nt, S], F32, name=f"wg{t}")
+                for g in range(4):
+                    nc.sync.dma_start(wt[32 * g : 32 * g + 32, :, :], wgs_q[:, t : t + nt, :])
+                for i in range(nt):
+                    wg[t + i] = wt[:, i, :]
+            pg = keep.tile([P, T2], F32, name=f"page{t}")
+            nc.sync.dma_start(pg[:], page0_t[t])
+            page.append(pg)
+            if t == 0:
+                nc.sync.dma_start(idx3[:], offs3)
+        w4_w = keep.tile([P, N], U32, name="w4_w", align_bytes=64)
+        nc.sync.dma_start(w4_w[:].bitcast(I32), w4_words[0].rearrange("p c i -> p (c i)").bitcast(I32))
+        for q in range(4):
+            nc.sync.dma_start(
+                w4_sc[32 * q : 32 * q + 4, :].bitcast(I32),
+                w4_scales[0, 4 * q : 4 * q + 4, :].bitcast(I32),
+            )
+
+        ident = keep.tile([P, P], F32, name="ident")
+        make_identity(nc, ident[:])
+
+        v_w, v_sc = [], []
+        for a in range(PASSES):
+            vw = keep.tile([P, S], U32, name=f"v_w{a}", align_bytes=64)
+            vs = keep.tile([P, S], U8, name=f"v_sc{a}", align_bytes=64)
+            if a == 0:
+                nc.vector.tensor_copy(vw[:], tab_w[a][:].indirect(idx1[:]))
+            nc.vector.tensor_copy(vs[:], tab_sc[:, a, :].indirect(idx1[:]))
+            if a == 1:
+                for half in range(2):
+                    nc.vector.tensor_copy(
+                        vw[:, half * BANK : (half + 1) * BANK],
+                        tab_w[a][:].indirect(idx1[:, half * 32 : (half + 1) * 32]),
+                    )
+            v_w.append(vw)
+            v_sc.append(vs)
+
+        w_codes = [[keep.tile([P, H], U32, name=f"wq{wi}{a}", align_bytes=64) for a in range(PASSES)] for wi in range(2)]
+        w_sc = [[keep.tile([P, H], U8, name=f"ws{wi}{a}", align_bytes=64) for a in range(PASSES)] for wi in range(2)]
+
+        def quantise_piece(n):
+            wi, a, c0, cn = pieces[n]
+            grouped = ring.tile([P, cn * PACK], BF16, name="grouped", tag="bf", bufs=6, align_bytes=64)
+            nc.vector.tensor_copy(
+                out=grouped[:].rearrange("p (c i t) -> p c t i", i=4, t=PACK),
+                in_=raws[n][:].rearrange("p t (c i) -> p c t i", i=4),
+            )
+            nc.vector.quantize_mx(
+                out=w_codes[wi][a][:, c0 : c0 + cn].bitcast(FP8X4),
+                scales=w_sc[wi][a][:, c0 : c0 + cn],
+                in_=grouped[:],
+            )
+
+        def product(jb, which):
+            acc = psum.tile([P, BANK], F32, name="acc", tag="acc", bufs=6)
+            cols = slice(jb * P, (jb + 1) * P)
+            for a in range(PASSES):
+                if which == 2:
+                    rhs, rhs_sc = w3_w[:, a, :].bitcast(FP4X4), w3_sc[:, a, :]
+                else:
+                    rhs, rhs_sc = w_codes[which][a][:].bitcast(FP8X4), w_sc[which][a][:]
+                nc.tensor.matmul_mx(
+                    out=acc[:], lhsT=v_w[a][:, cols].bitcast(FP8X4), lhsT_scale=v_sc[a][:, cols],
+                    rhs=rhs, rhs_scale=rhs_sc, start=(a == 0), stop=(a == PASSES - 1),
+                )
+            return acc[:].rearrange("p (m t) -> p t m", t=PACK)
+
+        neg_c = [keep.tile([P, PACK, P], F32, name=f"negc{jb}") for jb in range(JB)]
+        top = [keep.tile([P, PACK, P], F32, name=f"top{jb}") for jb in range(JB)]
+        h0 = keep.tile([P, S], F32, name="h0")
+        y01 = keep.tile([P, 2, S], F32, name="y01")
+        y23 = keep.tile([P, 2, S], F32, name="y23")
+        h = [h0[:], y01[:, 0, :], y01[:, 1, :], y23[:, 0, :]]
+        picked = [y01[:, 0, :], y01[:, 1, :], y23[:, 0, :], y23[:, 1, :]]
+
+        def turn(t, half):
+            bank = psum.tile([P, BANK], F32, name="ht", tag="ht", bufs=2)
+            for i in range(4):
+                jb = 4 * half + i
+                o = bank[:, i * P : (i + 1) * P]
+                nc.tensor.matmul(o, top[jb][:, t, :], ident[:], start=True, stop=False, is_transpose=True)
+                nc.tensor.matmul(o, neg_c[jb][:, t, :], ident[:], start=False, stop=True, is_transpose=True)
+            nc.scalar.activation(
+                h[t][:, half * BANK : (half + 1) * BANK], bank[:], ACT.Copy, scale=gain_sb[:, t : t + 1]
+            )
+
+        for half in range(2):
+            blocks = range(4 * half, 4 * half + 4)
+            for jb in blocks:
+                nc.scalar.activation(neg_c[jb][:], product(jb, 2), ACT.Copy, scale=-1.0)
+            if half == 0:
+                quantise_piece(0)
+                quantise_piece(1)
+            for jb in blocks:
+                nc.scalar.copy(top[jb][:], product(jb, 0))
+            if half == 0:
+                for n in range(2, len(pieces)):
+                    quantise_piece(n)
+            for jb in blocks:
+                nc.vector.tensor_tensor(top[jb][:], top[jb][:], product(jb, 1), ALU.max)
+            turn(0, half)
+            cols = slice(half * BANK, (half + 1) * BANK)
+            nc.vector.tensor_tensor(
+                page[0][:].indirect(idx2[:, half * 32 : (half + 1) * 32]), h[0][:, cols], wg[0][:, cols], ALU.mult
+            )
+        for t in range(1, PACK):
+            for half in range(2):
+                turn(t, half)
+
+        mnt_sb = []
+        for n in range(N // P):
+            mt = ring.tile([P, M], F32, name="mnt_sb", tag="raw", bufs=3)
+            nc.sync.dma_start(mt[:], mnt[n * P : (n + 1) * P, :])
+            mnt_sb.append(mt)
+
+        rounded = [ring.tile([P, BANK, PACK], BF16, name="rounded", tag="bf", bufs=6, align_bytes=64) for c in range(CHUNKS)]
+        x_bf = [ring.tile([P, BANK, PACK], BF16, name="x_bf", tag="bf", bufs=6, align_bytes=64) for c in range(2)]
+
+        def scatter(t):
+            if t > 0:
+                nc.vector.tensor_tensor(page[t][:].indirect(idx2[:]), h[t], wg[t], ALU.mult)
+            nc.sync.dma_start(out1_t[t], page[t][:])
+
+        def round_page(t, c):
+            nc.scalar.copy(rounded[c][:, :, t], page[t][:, c * BANK : (c + 1) * BANK])
+
+        def gather(t):
+            if t == 3:
+                for half in range(2):
+                    nc.vector.tensor_copy(
+                        picked[t][:, half * BANK : (half + 1) * BANK],
+                        page[t][:].indirect(idx3[:, half * 32 : (half + 1) * 32]),
+                    )
+            else:
+                nc.vector.tensor_copy(picked[t], page[t][:].indirect(idx3[:]))
+
+        def absolute(u, half):
+            src = (y01, y23)[u][:, :, half * BANK : (half + 1) * BANK]
+            nc.scalar.activation(x_bf[half][:, :, 2 * u : 2 * u + 2], src.rearrange("p e m -> p m e"), ACT.Abs)
+
+        for t in range(PACK):
+            scatter(t)
+            if t > 0:
+                gather(t - 1)
+            if t == 2:
+                absolute(0, 0)
+                absolute(0, 1)
+            if t < 3:
+                for c in range(CHUNKS):
+                    round_page(t, c)
+        gather(3)
+
+        p_codes = keep.tile([P, T2], U32, name="p_codes", align_bytes=64)
+        p_sc = keep.tile([P, T2], U8, name="p_sc", align_bytes=64)
+        out2_w = out_2[0].rearrange("p m i -> p (m i)").bitcast(I32)
+
+        def planes(c):
+            cols = slice(c * BANK, (c + 1) * BANK)
+            round_page(3, c)
+            nc.vector.quantize_mx(
+                out=p_codes[:, cols].bitcast(FP8X4), scales=p_sc[:, cols],
+                in_=rounded[c][:].rearrange("p m t -> p (m t)"),
+            )
+            nc.sync.dma_start(out2_w[:, cols], p_codes[:, cols].bitcast(I32))
+
+        def second_stage(half):
+            cols = slice(half * BANK, (half + 1) * BANK)
+            absolute(1, half)
+            x_codes = keep.tile([P, BANK], U32, name=f"x_codes{half}", align_bytes=64)
+            x_sc = keep.tile([P, BANK], U8, name=f"x_sc{half}", align_bytes=64)
+            nc.vector.quantize_mx(
+                out=x_codes[:].bitcast(FP8X4), scales=x_sc[:], in_=x_bf[half][:].rearrange("p m t -> p (m t)")
+            )
+            for n in range(N // P):
+                acc = psum.tile([P, BANK], F32, name="acc", tag="acc", bufs=6)
+                nc.tensor.matmul_mx(
+                    out=acc[:], lhsT=w4_w[:, n * P : (n + 1) * P].bitcast(FP8X4), lhsT_scale=w4_sc[:, n * P : (n + 1) * P],
+                    rhs=x_codes[:].bitcast(FP8X4), rhs_scale=x_sc[:], start=True, stop=True,
+                )
+                nc.vector.tensor_tensor(mnt_sb[n][:, cols], acc[:], mnt_sb[n][:, cols], ALU.add)
+                nc.sync.dma_start(out_0[n * P : (n + 1) * P, cols], mnt_sb[n][:, cols])
+
+        second_stage(0)
+        second_stage(1)
+        for c in range(CHUNKS):
+            planes(c)
+        for q in range(4):
+            (nc.scalar, nc.sync)[q % 2].dma_start(
+                out_3[0, 4 * q : 4 * q + 4, :].bitcast(I32), p_sc[32 * q : 32 * q + 4, :].bitcast(I32)
+            )

@@ -49,19 +49,19 @@ def tile_list_chord_span_archive_kernel(
         nc.vector.memset(w4_sc[:].bitcast(I32), 0)
 
         nc.sync.dma_start(idx1[:], offs)
-        tab_w = []
-        for a in range(PASSES):
-            tw = keep.tile([P, T], U32, name=f"tab_w{a}")
+        tab_w = [keep.tile([P, T], U32, name=f"tab_w{a}") for a in range(PASSES)]
+        tab_src = [tab_words[a].rearrange("p t i -> p (t i)").bitcast(I32) for a in range(PASSES)]
+        nc.sync.dma_start(tab_w[0][:, : T // 2].bitcast(I32), tab_src[0][:, : T // 2])
+        gain_sb = keep.tile([P, PACK], F32, name="gain_sb")
+        nc.sync.dma_start(idx2[:], offs2)
+        nc.sync.dma_start(idx3[:], offs3)
+        nc.sync.dma_start(gain_sb[:], gain.rearrange("(p t) -> p t", t=PACK))
+        for q in range(4):
             nc.sync.dma_start(
-                tw[:].bitcast(I32), tab_words[a].rearrange("p t i -> p (t i)").bitcast(I32)
+                tab_sc[32 * q : 32 * q + 4, :, :].bitcast(I32),
+                tab_scales[:, 4 * q : 4 * q + 4, :].rearrange("a r c -> r a c").bitcast(I32),
             )
-            tab_w.append(tw)
-            if a == 0:
-                for q in range(4):
-                    nc.sync.dma_start(
-                        tab_sc[32 * q : 32 * q + 4, :, :].bitcast(I32),
-                        tab_scales[:, 4 * q : 4 * q + 4, :].rearrange("a r c -> r a c").bitcast(I32),
-                    )
+        nc.sync.dma_start(tab_w[0][:, T // 2 :].bitcast(I32), tab_src[0][:, T // 2 :])
         w3_w = keep.tile([P, PASSES, 2 * H], U8, name="w3_w", align_bytes=64)
         nc.sync.dma_start(w3_w[:].bitcast(I32), w3_words.rearrange("a p c -> p a c").bitcast(I32))
         for q in range(4):
@@ -69,6 +69,7 @@ def tile_list_chord_span_archive_kernel(
                 w3_sc[32 * q : 32 * q + 4, :, :].bitcast(I32),
                 w3_scales[:, 4 * q : 4 * q + 4, :].rearrange("a r c -> r a c").bitcast(I32),
             )
+        nc.sync.dma_start(tab_w[1][:].bitcast(I32), tab_src[1])
 
         pieces = [(0, 0, 0, H), (0, 1, 0, H), (1, 0, 0, H), (1, 1, 0, H // 2), (1, 1, H // 2, H // 2)]
         raws = []
@@ -78,9 +79,6 @@ def tile_list_chord_span_archive_kernel(
             nc.sync.dma_start(raw[:], rows.rearrange("(p j) c -> p j c", j=PACK))
             raws.append(raw)
 
-        gain_sb = keep.tile([P, PACK], F32, name="gain_sb")
-        nc.sync.dma_start(gain_sb[:], gain.rearrange("(p t) -> p t", t=PACK))
-        nc.sync.dma_start(idx2[:], offs2)
         wgs_q = wgs.rearrange("(q t) j -> q t j", t=PACK)
         page0_t = page0.rearrange("(p t) m -> t p m", t=PACK)
         out1_t = out_1.rearrange("(p t) m -> t p m", t=PACK)
@@ -90,15 +88,13 @@ def tile_list_chord_span_archive_kernel(
             if t != 3:
                 nt = 2 if t == 2 else 1
                 wt = keep.tile([P, nt, S], F32, name=f"wg{t}")
-                for g in range(4):
+                for g in (0, 2, 1, 3):
                     nc.sync.dma_start(wt[32 * g : 32 * g + 32, :, :], wgs_q[:, t : t + nt, :])
                 for i in range(nt):
                     wg[t + i] = wt[:, i, :]
             pg = keep.tile([P, T2], F32, name=f"page{t}")
             nc.sync.dma_start(pg[:], page0_t[t])
             page.append(pg)
-            if t == 0:
-                nc.sync.dma_start(idx3[:], offs3)
         w4_w = keep.tile([P, N], U32, name="w4_w", align_bytes=64)
         nc.sync.dma_start(w4_w[:].bitcast(I32), w4_words[0].rearrange("p c i -> p (c i)").bitcast(I32))
         for q in range(4):
@@ -110,28 +106,23 @@ def tile_list_chord_span_archive_kernel(
         ident = keep.tile([P, P], F32, name="ident")
         make_identity(nc, ident[:])
 
-        v_w, v_sc = [], []
+        v_w = [keep.tile([P, S], U32, name=f"v_w{a}", align_bytes=64) for a in range(PASSES)]
+        v_sc = [keep.tile([P, S], U8, name=f"v_sc{a}", align_bytes=64) for a in range(PASSES)]
         for a in range(PASSES):
-            vw = keep.tile([P, S], U32, name=f"v_w{a}", align_bytes=64)
-            vs = keep.tile([P, S], U8, name=f"v_sc{a}", align_bytes=64)
-            if a == 0:
-                nc.vector.tensor_copy(vw[:], tab_w[a][:].indirect(idx1[:]))
-            nc.vector.tensor_copy(vs[:], tab_sc[:, a, :].indirect(idx1[:]))
-            if a == 1:
-                for half in range(2):
-                    nc.vector.tensor_copy(
-                        vw[:, half * BANK : (half + 1) * BANK],
-                        tab_w[a][:].indirect(idx1[:, half * 32 : (half + 1) * 32]),
-                    )
-            v_w.append(vw)
-            v_sc.append(vs)
+            nc.vector.tensor_copy(v_sc[a][:], tab_sc[:, a, :].indirect(idx1[:]))
+        nc.vector.tensor_copy(v_w[0][:], tab_w[0][:].indirect(idx1[:]))
+        for half in range(2):
+            nc.vector.tensor_copy(
+                v_w[1][:, half * BANK : (half + 1) * BANK],
+                tab_w[1][:].indirect(idx1[:, half * 32 : (half + 1) * 32]),
+            )
 
         w_codes = [[keep.tile([P, H], U32, name=f"wq{wi}{a}", align_bytes=64) for a in range(PASSES)] for wi in range(2)]
         w_sc = [[keep.tile([P, H], U8, name=f"ws{wi}{a}", align_bytes=64) for a in range(PASSES)] for wi in range(2)]
 
         def quantise_piece(n):
             wi, a, c0, cn = pieces[n]
-            grouped = ring.tile([P, cn * PACK], BF16, name="grouped", tag="bf", bufs=6, align_bytes=64)
+            grouped = ring.tile([P, cn * PACK], BF16, name="grouped", tag="bf", bufs=5, align_bytes=64)
             nc.vector.tensor_copy(
                 out=grouped[:].rearrange("p (c i t) -> p c t i", i=4, t=PACK),
                 in_=raws[n][:].rearrange("p t (c i) -> p c t i", i=4),
@@ -156,29 +147,33 @@ def tile_list_chord_span_archive_kernel(
                 )
             return acc[:].rearrange("p (m t) -> p t m", t=PACK)
 
-        neg_c = [keep.tile([P, PACK, P], F32, name=f"negc{jb}") for jb in range(JB)]
+        neg_c = [ring.tile([P, 4, PACK, P], F32, name="neg_c", tag="cf", bufs=2) for half in range(2)]
         top = [keep.tile([P, PACK, P], F32, name=f"top{jb}") for jb in range(JB)]
         h0 = keep.tile([P, S], F32, name="h0")
+        h2 = keep.tile([P, S], F32, name="h2")
         y01 = keep.tile([P, 2, S], F32, name="y01")
         y23 = keep.tile([P, 2, S], F32, name="y23")
-        h = [h0[:], y01[:, 0, :], y01[:, 1, :], y23[:, 0, :]]
+        h = [h0[:], y01[:, 0, :], h2[:], y23[:, 0, :]]
         picked = [y01[:, 0, :], y01[:, 1, :], y23[:, 0, :], y23[:, 1, :]]
 
-        def turn(t, half):
-            bank = psum.tile([P, BANK], F32, name="ht", tag="ht", bufs=2)
-            for i in range(4):
-                jb = 4 * half + i
-                o = bank[:, i * P : (i + 1) * P]
-                nc.tensor.matmul(o, top[jb][:, t, :], ident[:], start=True, stop=False, is_transpose=True)
-                nc.tensor.matmul(o, neg_c[jb][:, t, :], ident[:], start=False, stop=True, is_transpose=True)
-            nc.scalar.activation(
-                h[t][:, half * BANK : (half + 1) * BANK], bank[:], ACT.Copy, scale=gain_sb[:, t : t + 1]
-            )
+        def dealt(ap):
+            return ap.rearrange("p (t m) -> p t m", t=PACK)
+
+        larger = [top[0][:], top[1][:], top[2][:], top[3][:], dealt(wg[0][:, :BANK]), dealt(h0[:, :BANK]), top[4][:], top[5][:]]
+
+        def turn(t, blocks, dst):
+            bank = psum.tile([P, 4, P], F32, name="ht", tag="ht", bufs=2)
+            for i in reversed(range(len(blocks))):
+                jb = blocks[i]
+                o = bank[:, i, :]
+                nc.tensor.matmul(o, larger[jb][:, t, :], ident[:], start=True, stop=False, is_transpose=True)
+                nc.tensor.matmul(o, neg_c[jb // 4][:, jb % 4, t, :], ident[:], start=False, stop=True, is_transpose=True)
+            nc.scalar.activation(dst, bank[:, : len(blocks), :], ACT.Copy, scale=gain_sb[:, t : t + 1])
 
         for half in range(2):
             blocks = range(4 * half, 4 * half + 4)
             for jb in blocks:
-                nc.scalar.activation(neg_c[jb][:], product(jb, 2), ACT.Copy, scale=-1.0)
+                nc.scalar.activation(neg_c[half][:, jb % 4, :, :], product(jb, 2), ACT.Copy, scale=-1.0)
             if half == 0:
                 quantise_piece(0)
                 quantise_piece(1)
@@ -188,15 +183,16 @@ def tile_list_chord_span_archive_kernel(
                 for n in range(2, len(pieces)):
                     quantise_piece(n)
             for jb in blocks:
-                nc.vector.tensor_tensor(top[jb][:], top[jb][:], product(jb, 1), ALU.max)
-            turn(0, half)
-            cols = slice(half * BANK, (half + 1) * BANK)
-            nc.vector.tensor_tensor(
-                page[0][:].indirect(idx2[:, half * 32 : (half + 1) * 32]), h[0][:, cols], wg[0][:, cols], ALU.mult
-            )
+                nc.vector.tensor_tensor(larger[jb], top[jb][:], product(jb, 1), ALU.max)
+            for jb0 in (4 * half, 4 * half + 2):
+                cols = slice(jb0 * P, (jb0 + 2) * P)
+                turn(0, [jb0, jb0 + 1], h[0][:, cols].rearrange("p (i c) -> p i c", c=P))
+                nc.vector.tensor_tensor(
+                    page[0][:].indirect(idx2[:, jb0 * 8 : (jb0 + 2) * 8]), h[0][:, cols], wg[0][:, cols], ALU.mult
+                )
         for t in range(1, PACK):
-            for half in range(2):
-                turn(t, half)
+            for e in range(2):
+                turn(t, list(range(e, JB, 2)), h[t].rearrange("p (i e c) -> p e i c", e=2, c=P)[:, e, :, :])
 
         mnt_sb = []
         for n in range(N // P):
@@ -204,42 +200,46 @@ def tile_list_chord_span_archive_kernel(
             nc.sync.dma_start(mt[:], mnt[n * P : (n + 1) * P, :])
             mnt_sb.append(mt)
 
-        rounded = [ring.tile([P, BANK, PACK], BF16, name="rounded", tag="bf", bufs=6, align_bytes=64) for c in range(CHUNKS)]
-        x_bf = [ring.tile([P, BANK, PACK], BF16, name="x_bf", tag="bf", bufs=6, align_bytes=64) for c in range(2)]
+        pairs = [ring.tile([P, 2, T2 // 2], U32, name="pairs", tag="cf", bufs=2) for half in range(2)]
+        x_bf = [ring.tile([P, BANK, PACK], BF16, name="x_bf", tag="bf", bufs=5, align_bytes=64) for c in range(2)]
 
         def scatter(t):
             if t > 0:
                 nc.vector.tensor_tensor(page[t][:].indirect(idx2[:]), h[t], wg[t], ALU.mult)
             nc.sync.dma_start(out1_t[t], page[t][:])
 
-        def round_page(t, c):
-            nc.scalar.copy(rounded[c][:, :, t], page[t][:, c * BANK : (c + 1) * BANK])
+        def round_page(t, half):
+            dst = pairs[half][:, t // 2, :].bitcast(BF16).rearrange("p (m e) -> p m e", e=2)
+            nc.scalar.copy(dst[:, :, t % 2], page[t][:, half * (T2 // 2) : (half + 1) * (T2 // 2)])
 
         def gather(t):
-            if t == 3:
-                for half in range(2):
-                    nc.vector.tensor_copy(
-                        picked[t][:, half * BANK : (half + 1) * BANK],
-                        page[t][:].indirect(idx3[:, half * 32 : (half + 1) * 32]),
-                    )
-            else:
-                nc.vector.tensor_copy(picked[t], page[t][:].indirect(idx3[:]))
+            nc.vector.tensor_copy(picked[t], page[t][:].indirect(idx3[:]))
+
+        def gather_half(t, half):
+            nc.vector.tensor_copy(
+                picked[t][:, half * BANK : (half + 1) * BANK],
+                page[t][:].indirect(idx3[:, half * 32 : (half + 1) * 32]),
+            )
 
         def absolute(u, half):
             src = (y01, y23)[u][:, :, half * BANK : (half + 1) * BANK]
             nc.scalar.activation(x_bf[half][:, :, 2 * u : 2 * u + 2], src.rearrange("p e m -> p m e"), ACT.Abs)
 
-        for t in range(PACK):
-            scatter(t)
-            if t > 0:
-                gather(t - 1)
-            if t == 2:
+        scatter(0)
+        scatter(1)
+        gather(0)
+        gather(1)
+        scatter(2)
+        scatter(3)
+        for half in range(2):
+            gather_half(2, half)
+            gather_half(3, half)
+        for t in range(3):
+            for half in range(2):
+                round_page(t, half)
+            if t == 1:
                 absolute(0, 0)
                 absolute(0, 1)
-            if t < 3:
-                for c in range(CHUNKS):
-                    round_page(t, c)
-        gather(3)
 
         p_codes = keep.tile([P, T2], U32, name="p_codes", align_bytes=64)
         p_sc = keep.tile([P, T2], U8, name="p_sc", align_bytes=64)
@@ -247,12 +247,21 @@ def tile_list_chord_span_archive_kernel(
 
         def planes(c):
             cols = slice(c * BANK, (c + 1) * BANK)
-            round_page(3, c)
+            rounded = ring.tile([P, BANK, 2], U32, name="rounded", tag="bf", bufs=5, align_bytes=64)
+            src = pairs[c // 2][:, :, (c % 2) * BANK : (c % 2 + 1) * BANK]
+            nc.scalar.copy(rounded[:], src.rearrange("p u m -> p m u"))
             nc.vector.quantize_mx(
                 out=p_codes[:, cols].bitcast(FP8X4), scales=p_sc[:, cols],
-                in_=rounded[c][:].rearrange("p m t -> p (m t)"),
+                in_=rounded[:].rearrange("p m u -> p (m u)").bitcast(BF16),
             )
             nc.sync.dma_start(out2_w[:, cols], p_codes[:, cols].bitcast(I32))
+
+        def plane_scales(half):
+            cols = slice(half * (T2 // 2), (half + 1) * (T2 // 2))
+            for q in range(4):
+                (nc.sync, nc.scalar)[half * (q % 2)].dma_start(
+                    out_3[0, 4 * q : 4 * q + 4, cols].bitcast(I32), p_sc[32 * q : 32 * q + 4, cols].bitcast(I32)
+                )
 
         def second_stage(half):
             cols = slice(half * BANK, (half + 1) * BANK)
@@ -271,11 +280,13 @@ def tile_list_chord_span_archive_kernel(
                 nc.vector.tensor_tensor(mnt_sb[n][:, cols], acc[:], mnt_sb[n][:, cols], ALU.add)
                 nc.sync.dma_start(out_0[n * P : (n + 1) * P, cols], mnt_sb[n][:, cols])
 
+        round_page(3, 0)
         second_stage(0)
+        planes(0)
         second_stage(1)
-        for c in range(CHUNKS):
-            planes(c)
-        for q in range(4):
-            (nc.scalar, nc.sync)[q % 2].dma_start(
-                out_3[0, 4 * q : 4 * q + 4, :].bitcast(I32), p_sc[32 * q : 32 * q + 4, :].bitcast(I32)
-            )
+        planes(1)
+        plane_scales(0)
+        round_page(3, 1)
+        planes(2)
+        planes(3)
+        plane_scales(1)

@@ -40,26 +40,26 @@ def tile_list_chord_span_archive_kernel(
         idx2 = lists.tile([P, S // 16], U16, name="idx2")
         idx3 = lists.tile([P, M // 16], U16, name="idx3")
 
-        tab_sc = keep.tile([P, PASSES, T], U8, name="tab_sc", align_bytes=64)
+        tab_sc = keep.tile([P, T], U8, name="tab_sc", align_bytes=64)
+        v_sc1 = keep.tile([P, S], U8, name="v_sc1", align_bytes=64)
         w3_sc = keep.tile([P, PASSES, H], U8, name="w3_sc", align_bytes=64)
         w4_sc = keep.tile([P, N], U8, name="w4_sc", align_bytes=64)
-        nc.vector.memset(tab_sc[:, 0, :].bitcast(I32), 0)
-        nc.gpsimd.memset(tab_sc[:, 1, :].bitcast(I32), 0)
+        nc.vector.memset(tab_sc[:, : T // 2].bitcast(I32), 0)
+        nc.gpsimd.memset(tab_sc[:, T // 2 :].bitcast(I32), 0)
         nc.vector.memset(w3_sc[:].bitcast(I32), 0)
+        nc.vector.memset(v_sc1[:].bitcast(I32), 0)
         nc.vector.memset(w4_sc[:].bitcast(I32), 0)
 
         nc.sync.dma_start(idx1[:], offs)
         tab_w = [keep.tile([P, T], U32, name=f"tab_w{a}") for a in range(PASSES)]
         tab_src = [tab_words[a].rearrange("p t i -> p (t i)").bitcast(I32) for a in range(PASSES)]
         nc.sync.dma_start(tab_w[0][:, : T // 2].bitcast(I32), tab_src[0][:, : T // 2])
-        gain_sb = keep.tile([P, PACK], F32, name="gain_sb")
         nc.sync.dma_start(idx2[:], offs2)
         nc.sync.dma_start(idx3[:], offs3)
-        nc.sync.dma_start(gain_sb[:], gain.rearrange("(p t) -> p t", t=PACK))
         for q in range(4):
             nc.sync.dma_start(
-                tab_sc[32 * q : 32 * q + 4, :, :].bitcast(I32),
-                tab_scales[:, 4 * q : 4 * q + 4, :].rearrange("a r c -> r a c").bitcast(I32),
+                tab_sc[32 * q : 32 * q + 4 * PASSES, :].bitcast(I32),
+                tab_scales[:, 4 * q : 4 * q + 4, :].bitcast(I32),
             )
         nc.sync.dma_start(tab_w[0][:, T // 2 :].bitcast(I32), tab_src[0][:, T // 2 :])
         w3_w = keep.tile([P, PASSES, 2 * H], U8, name="w3_w", align_bytes=64)
@@ -70,6 +70,12 @@ def tile_list_chord_span_archive_kernel(
                 w3_scales[:, 4 * q : 4 * q + 4, :].rearrange("a r c -> r a c").bitcast(I32),
             )
         nc.sync.dma_start(tab_w[1][:].bitcast(I32), tab_src[1])
+        v_sc = keep.tile([P, S], U8, name="v_sc", align_bytes=64)
+        nc.vector.tensor_copy(v_sc[:], tab_sc[:].indirect(idx1[:]))
+        for q in range(4):
+            nc.sync.dma_start(
+                v_sc1[32 * q : 32 * q + 4, :].bitcast(I32), v_sc[32 * q + 4 : 32 * q + 8, :].bitcast(I32)
+            )
 
         pieces = [(0, 0, 0, H), (0, 1, 0, H), (1, 0, 0, H), (1, 1, 0, H // 2), (1, 1, H // 2, H // 2)]
         raws = []
@@ -79,6 +85,8 @@ def tile_list_chord_span_archive_kernel(
             nc.sync.dma_start(raw[:], rows.rearrange("(p j) c -> p j c", j=PACK))
             raws.append(raw)
 
+        gain_sb = keep.tile([P, PACK], F32, name="gain_sb")
+        nc.sync.dma_start(gain_sb[:], gain.rearrange("(p t) -> p t", t=PACK))
         wgs_q = wgs.rearrange("(q t) j -> q t j", t=PACK)
         page0_t = page0.rearrange("(p t) m -> t p m", t=PACK)
         out1_t = out_1.rearrange("(p t) m -> t p m", t=PACK)
@@ -107,9 +115,6 @@ def tile_list_chord_span_archive_kernel(
         make_identity(nc, ident[:])
 
         v_w = [keep.tile([P, S], U32, name=f"v_w{a}", align_bytes=64) for a in range(PASSES)]
-        v_sc = [keep.tile([P, S], U8, name=f"v_sc{a}", align_bytes=64) for a in range(PASSES)]
-        for a in range(PASSES):
-            nc.vector.tensor_copy(v_sc[a][:], tab_sc[:, a, :].indirect(idx1[:]))
         nc.vector.tensor_copy(v_w[0][:], tab_w[0][:].indirect(idx1[:]))
         for half in range(2):
             nc.vector.tensor_copy(
@@ -139,10 +144,12 @@ def tile_list_chord_span_archive_kernel(
             for a in range(PASSES):
                 if which == 2:
                     rhs, rhs_sc = w3_w[:, a, :].bitcast(FP4X4), w3_sc[:, a, :]
+                    lhs_sc = (v_sc, v_sc1)[a][:, cols]
                 else:
                     rhs, rhs_sc = w_codes[which][a][:].bitcast(FP8X4), w_sc[which][a][:]
+                    lhs_sc = v_sc[4 * a :, cols]
                 nc.tensor.matmul_mx(
-                    out=acc[:], lhsT=v_w[a][:, cols].bitcast(FP8X4), lhsT_scale=v_sc[a][:, cols],
+                    out=acc[:], lhsT=v_w[a][:, cols].bitcast(FP8X4), lhsT_scale=lhs_sc,
                     rhs=rhs, rhs_scale=rhs_sc, start=(a == 0), stop=(a == PASSES - 1),
                 )
             return acc[:].rearrange("p (m t) -> p t m", t=PACK)
@@ -259,7 +266,7 @@ def tile_list_chord_span_archive_kernel(
         def plane_scales(half):
             cols = slice(half * (T2 // 2), (half + 1) * (T2 // 2))
             for q in range(4):
-                (nc.sync, nc.scalar)[half * (q % 2)].dma_start(
+                nc.sync.dma_start(
                     out_3[0, 4 * q : 4 * q + 4, cols].bitcast(I32), p_sc[32 * q : 32 * q + 4, cols].bitcast(I32)
                 )
 

@@ -55,12 +55,12 @@ def tile_list_chord_span_archive_kernel(
         tab_src = [tab_words[a].rearrange("p t i -> p (t i)").bitcast(I32) for a in range(PASSES)]
         nc.sync.dma_start(tab_w[0][:, : T // 2].bitcast(I32), tab_src[0][:, : T // 2])
         nc.sync.dma_start(idx2[:], offs2)
-        nc.sync.dma_start(idx3[:], offs3)
         for q in range(4):
             nc.sync.dma_start(
-                tab_sc[32 * q : 32 * q + 4 * PASSES, :].bitcast(I32),
-                tab_scales[:, 4 * q : 4 * q + 4, :].bitcast(I32),
+                tab_sc[32 * q : 32 * q + 4, :].bitcast(I32),
+                tab_scales[0, 4 * q : 4 * q + 4, :].bitcast(I32),
             )
+        nc.sync.dma_start(tab_sc[8:24, :].bitcast(I32), tab_scales[1].bitcast(I32))
         nc.sync.dma_start(tab_w[0][:, T // 2 :].bitcast(I32), tab_src[0][:, T // 2 :])
         w3_w = keep.tile([P, PASSES, 2 * H], U8, name="w3_w", align_bytes=64)
         nc.sync.dma_start(w3_w[:].bitcast(I32), w3_words.rearrange("a p c -> p a c").bitcast(I32))
@@ -74,7 +74,7 @@ def tile_list_chord_span_archive_kernel(
         nc.vector.tensor_copy(v_sc[:], tab_sc[:].indirect(idx1[:]))
         for q in range(4):
             nc.sync.dma_start(
-                v_sc1[32 * q : 32 * q + 4, :].bitcast(I32), v_sc[32 * q + 4 : 32 * q + 8, :].bitcast(I32)
+                v_sc1[32 * q : 32 * q + 4, :].bitcast(I32), v_sc[8 + 4 * q : 12 + 4 * q, :].bitcast(I32)
             )
 
         pieces = [(0, 0, 0, H), (0, 1, 0, H), (1, 0, 0, H), (1, 1, 0, H // 2), (1, 1, H // 2, H // 2)]
@@ -87,6 +87,7 @@ def tile_list_chord_span_archive_kernel(
 
         gain_sb = keep.tile([P, PACK], F32, name="gain_sb")
         nc.sync.dma_start(gain_sb[:], gain.rearrange("(p t) -> p t", t=PACK))
+        nc.sync.dma_start(idx3[:], offs3)
         wgs_q = wgs.rearrange("(q t) j -> q t j", t=PACK)
         page0_t = page0.rearrange("(p t) m -> t p m", t=PACK)
         out1_t = out_1.rearrange("(p t) m -> t p m", t=PACK)
@@ -125,17 +126,17 @@ def tile_list_chord_span_archive_kernel(
         w_codes = [[keep.tile([P, H], U32, name=f"wq{wi}{a}", align_bytes=64) for a in range(PASSES)] for wi in range(2)]
         w_sc = [[keep.tile([P, H], U8, name=f"ws{wi}{a}", align_bytes=64) for a in range(PASSES)] for wi in range(2)]
 
-        def quantise_piece(n):
-            wi, a, c0, cn = pieces[n]
-            grouped = ring.tile([P, cn * PACK], BF16, name="grouped", tag="bf", bufs=5, align_bytes=64)
-            nc.vector.tensor_copy(
-                out=grouped[:].rearrange("p (c i t) -> p c t i", i=4, t=PACK),
-                in_=raws[n][:].rearrange("p t (c i) -> p c t i", i=4),
-            )
+        def quantise_weight(wi, a):
+            grouped = ring.tile([P, PACK, P, PACK], BF16, name="grouped", tag="bf", bufs=5, align_bytes=64)
+            for raw, (pw, pa, c0, cn) in zip(raws, pieces):
+                if (pw, pa) == (wi, a):
+                    nc.vector.tensor_copy(
+                        out=grouped[:, :, c0 // PACK : (c0 + cn) // PACK, :].rearrange("p t m i -> p m i t"),
+                        in_=raw[:].rearrange("p i (m t) -> p m i t", t=PACK),
+                    )
             nc.vector.quantize_mx(
-                out=w_codes[wi][a][:, c0 : c0 + cn].bitcast(FP8X4),
-                scales=w_sc[wi][a][:, c0 : c0 + cn],
-                in_=grouped[:],
+                out=w_codes[wi][a][:].bitcast(FP8X4), scales=w_sc[wi][a][:],
+                in_=grouped[:].rearrange("p t m i -> p (t m i)"),
             )
 
         def product(jb, which):
@@ -144,15 +145,13 @@ def tile_list_chord_span_archive_kernel(
             for a in range(PASSES):
                 if which == 2:
                     rhs, rhs_sc = w3_w[:, a, :].bitcast(FP4X4), w3_sc[:, a, :]
-                    lhs_sc = (v_sc, v_sc1)[a][:, cols]
                 else:
                     rhs, rhs_sc = w_codes[which][a][:].bitcast(FP8X4), w_sc[which][a][:]
-                    lhs_sc = v_sc[4 * a :, cols]
                 nc.tensor.matmul_mx(
-                    out=acc[:], lhsT=v_w[a][:, cols].bitcast(FP8X4), lhsT_scale=lhs_sc,
+                    out=acc[:], lhsT=v_w[a][:, cols].bitcast(FP8X4), lhsT_scale=(v_sc, v_sc1)[a][:, cols],
                     rhs=rhs, rhs_scale=rhs_sc, start=(a == 0), stop=(a == PASSES - 1),
                 )
-            return acc[:].rearrange("p (m t) -> p t m", t=PACK)
+            return acc
 
         neg_c = [ring.tile([P, 4, PACK, P], F32, name="neg_c", tag="cf", bufs=2) for half in range(2)]
         top = [keep.tile([P, PACK, P], F32, name=f"top{jb}") for jb in range(JB)]
@@ -180,17 +179,20 @@ def tile_list_chord_span_archive_kernel(
         for half in range(2):
             blocks = range(4 * half, 4 * half + 4)
             for jb in blocks:
-                nc.scalar.activation(neg_c[half][:, jb % 4, :, :], product(jb, 2), ACT.Copy, scale=-1.0)
+                nc.scalar.activation(
+                    neg_c[half][:, jb % 4, :, :].rearrange("p t m -> p m t"),
+                    product(jb, 2)[:].rearrange("p (m t) -> p m t", t=PACK), ACT.Copy, scale=-1.0,
+                )
             if half == 0:
-                quantise_piece(0)
-                quantise_piece(1)
+                quantise_weight(0, 0)
+                quantise_weight(0, 1)
             for jb in blocks:
-                nc.scalar.copy(top[jb][:], product(jb, 0))
+                nc.scalar.copy(top[jb][:], dealt(product(jb, 0)[:]))
             if half == 0:
-                for n in range(2, len(pieces)):
-                    quantise_piece(n)
+                quantise_weight(1, 0)
+                quantise_weight(1, 1)
             for jb in blocks:
-                nc.vector.tensor_tensor(larger[jb], top[jb][:], product(jb, 1), ALU.max)
+                nc.vector.tensor_tensor(larger[jb], top[jb][:], dealt(product(jb, 1)[:]), ALU.max)
             for jb0 in (4 * half, 4 * half + 2):
                 cols = slice(jb0 * P, (jb0 + 2) * P)
                 turn(0, [jb0, jb0 + 1], h[0][:, cols].rearrange("p (i c) -> p i c", c=P))

@@ -19,10 +19,17 @@ ALU = mybir.AluOpType
 
 P = 128
 PACK = 4
-PASSES = K // (P * PACK)
+K_PASS = P * PACK
+PASSES = K // K_PASS
 BANK = 512
-JB = S // P
+QUADRANTS = 4
+GROUP = 16
+BLOCKS = S // P
 CHUNKS = T2 // BANK
+SPARE_ROWS = 8
+SUM_BANKS = 6
+TURN_BANKS = 2
+BF16_SLOTS = 5
 
 
 def tile_list_chord_span_archive_kernel(
@@ -36,9 +43,15 @@ def tile_list_chord_span_archive_kernel(
         ring = ctx.enter_context(tc.tile_pool(name="ring", bufs=1))
         psum = ctx.enter_context(tc.psum_pool(name="psum", bufs=1))
 
-        idx1 = lists.tile([P, S // 16], U16, name="idx1")
-        idx2 = lists.tile([P, S // 16], U16, name="idx2")
-        idx3 = lists.tile([P, M // 16], U16, name="idx3")
+        idx1 = lists.tile([P, S // GROUP], U16, name="idx1")
+        idx2 = lists.tile([P, S // GROUP], U16, name="idx2")
+        idx3 = lists.tile([P, M // GROUP], U16, name="idx3")
+
+        def entries(idx, first, count):
+            return idx[:, first // GROUP : (first + count) // GROUP]
+
+        def live_rows(tile, q):
+            return tile[32 * q : 32 * q + 4].bitcast(I32)
 
         tab_sc = keep.tile([P, T], U8, name="tab_sc", align_bytes=64)
         v_sc1 = keep.tile([P, S], U8, name="v_sc1", align_bytes=64)
@@ -55,247 +68,242 @@ def tile_list_chord_span_archive_kernel(
         tab_src = [tab_words[a].rearrange("p t i -> p (t i)").bitcast(I32) for a in range(PASSES)]
         nc.sync.dma_start(tab_w[0][:, : T // 2].bitcast(I32), tab_src[0][:, : T // 2])
         nc.sync.dma_start(idx2[:], offs2)
-        for q in range(4):
-            nc.sync.dma_start(
-                tab_sc[32 * q : 32 * q + 4, :].bitcast(I32),
-                tab_scales[0, 4 * q : 4 * q + 4, :].bitcast(I32),
-            )
-        nc.sync.dma_start(tab_sc[8:24, :].bitcast(I32), tab_scales[1].bitcast(I32))
+        for q in range(QUADRANTS):
+            nc.sync.dma_start(live_rows(tab_sc, q), tab_scales[0, 4 * q : 4 * q + 4, :].bitcast(I32))
+        nc.sync.dma_start(tab_sc[SPARE_ROWS : SPARE_ROWS + 16, :].bitcast(I32), tab_scales[1].bitcast(I32))
         nc.sync.dma_start(tab_w[0][:, T // 2 :].bitcast(I32), tab_src[0][:, T // 2 :])
         w3_w = keep.tile([P, PASSES, 2 * H], U8, name="w3_w", align_bytes=64)
         nc.sync.dma_start(w3_w[:].bitcast(I32), w3_words.rearrange("a p c -> p a c").bitcast(I32))
-        for q in range(4):
+        for q in range(QUADRANTS):
             nc.sync.dma_start(
-                w3_sc[32 * q : 32 * q + 4, :, :].bitcast(I32),
-                w3_scales[:, 4 * q : 4 * q + 4, :].rearrange("a r c -> r a c").bitcast(I32),
+                live_rows(w3_sc, q), w3_scales[:, 4 * q : 4 * q + 4, :].rearrange("a s c -> s a c").bitcast(I32)
             )
         nc.sync.dma_start(tab_w[1][:].bitcast(I32), tab_src[1])
-        v_sc = keep.tile([P, S], U8, name="v_sc", align_bytes=64)
-        nc.vector.tensor_copy(v_sc[:], tab_sc[:].indirect(idx1[:]))
-        for q in range(4):
-            nc.sync.dma_start(
-                v_sc1[32 * q : 32 * q + 4, :].bitcast(I32), v_sc[8 + 4 * q : 12 + 4 * q, :].bitcast(I32)
-            )
+        v_sc0 = keep.tile([P, S], U8, name="v_sc0", align_bytes=64)
+        nc.vector.tensor_copy(v_sc0[:], tab_sc[:].indirect(idx1[:]))
+        for q in range(QUADRANTS):
+            first = SPARE_ROWS + 4 * q
+            nc.sync.dma_start(live_rows(v_sc1, q), v_sc0[first : first + 4, :].bitcast(I32))
+        v_sc = (v_sc0, v_sc1)
 
         pieces = [(0, 0, 0, H), (0, 1, 0, H), (1, 0, 0, H), (1, 1, 0, H // 2), (1, 1, H // 2, H // 2)]
         raws = []
-        for wi, a, c0, cn in pieces:
-            raw = ring.tile([P, PACK, cn], F32, name="raw", tag="raw" if cn == H else "rawh", bufs=3 if cn == H else 2)
-            rows = (w1, w2)[wi][a * 512 : (a + 1) * 512, c0 : c0 + cn]
-            nc.sync.dma_start(raw[:], rows.rearrange("(p j) c -> p j c", j=PACK))
+        for weight, a, c0, width in pieces:
+            whole = width == H
+            raw = ring.tile([P, PACK, width], F32, name="raw", tag="raw" if whole else "raw_half", bufs=3 if whole else 2)
+            rows = (w1, w2)[weight][a * K_PASS : (a + 1) * K_PASS, c0 : c0 + width]
+            nc.sync.dma_start(raw[:], rows.rearrange("(p i) c -> p i c", i=PACK))
             raws.append(raw)
 
         gain_sb = keep.tile([P, PACK], F32, name="gain_sb")
         nc.sync.dma_start(gain_sb[:], gain.rearrange("(p t) -> p t", t=PACK))
         nc.sync.dma_start(idx3[:], offs3)
-        wgs_q = wgs.rearrange("(q t) j -> q t j", t=PACK)
-        page0_t = page0.rearrange("(p t) m -> t p m", t=PACK)
-        out1_t = out_1.rearrange("(p t) m -> t p m", t=PACK)
-        wg = [None] * PACK
-        page = []
-        for t in range(PACK):
-            if t != 3:
-                nt = 2 if t == 2 else 1
-                wt = keep.tile([P, nt, S], F32, name=f"wg{t}")
-                for g in (0, 2, 1, 3):
-                    nc.sync.dma_start(wt[32 * g : 32 * g + 32, :, :], wgs_q[:, t : t + nt, :])
-                for i in range(nt):
-                    wg[t + i] = wt[:, i, :]
-            pg = keep.tile([P, T2], F32, name=f"page{t}")
-            nc.sync.dma_start(pg[:], page0_t[t])
-            page.append(pg)
+        page0_slices = page0.rearrange("(p t) m -> t p m", t=PACK)
+        out1_slices = out_1.rearrange("(p t) m -> t p m", t=PACK)
+        wgs_rows = wgs.rearrange("(u t) j -> u t j", t=PACK)
+
+        def load_page(t):
+            tile = keep.tile([P, T2], F32, name=f"page{t}")
+            nc.sync.dma_start(tile[:], page0_slices[t])
+            return tile
+
+        def load_factors(t, count, column_ranges):
+            tile = keep.tile([P, count, S], F32, name=f"factors{t}")
+            for cols in column_ranges:
+                for q in (0, 2, 1, 3):
+                    nc.sync.dma_start(tile[32 * q : 32 * q + 32, :, cols], wgs_rows[:, t : t + count, cols])
+            return [tile[:, i, :] for i in range(count)]
+
+        page = [load_page(0)]
+        factors = load_factors(0, 1, [slice(0, S // 2), slice(S // 2, S)])
+        factors.extend(load_factors(1, 1, [slice(0, S)]))
+        page.append(load_page(1))
+        factors.extend(load_factors(2, 2, [slice(0, S)]))
+        page.append(load_page(2))
+        page.append(load_page(3))
         w4_w = keep.tile([P, N], U32, name="w4_w", align_bytes=64)
         nc.sync.dma_start(w4_w[:].bitcast(I32), w4_words[0].rearrange("p c i -> p (c i)").bitcast(I32))
-        for q in range(4):
-            nc.sync.dma_start(
-                w4_sc[32 * q : 32 * q + 4, :].bitcast(I32),
-                w4_scales[0, 4 * q : 4 * q + 4, :].bitcast(I32),
-            )
+        for q in range(QUADRANTS):
+            nc.sync.dma_start(live_rows(w4_sc, q), w4_scales[0, 4 * q : 4 * q + 4, :].bitcast(I32))
 
         ident = keep.tile([P, P], F32, name="ident")
         make_identity(nc, ident[:])
 
         v_w = [keep.tile([P, S], U32, name=f"v_w{a}", align_bytes=64) for a in range(PASSES)]
         nc.vector.tensor_copy(v_w[0][:], tab_w[0][:].indirect(idx1[:]))
-        for half in range(2):
-            nc.vector.tensor_copy(
-                v_w[1][:, half * BANK : (half + 1) * BANK],
-                tab_w[1][:].indirect(idx1[:, half * 32 : (half + 1) * 32]),
-            )
+        for first in (0, S // 2):
+            nc.vector.tensor_copy(v_w[1][:, first : first + S // 2], tab_w[1][:].indirect(entries(idx1, first, S // 2)))
 
-        w_codes = [[keep.tile([P, H], U32, name=f"wq{wi}{a}", align_bytes=64) for a in range(PASSES)] for wi in range(2)]
-        w_sc = [[keep.tile([P, H], U8, name=f"ws{wi}{a}", align_bytes=64) for a in range(PASSES)] for wi in range(2)]
+        w_codes = [[keep.tile([P, H], U32, name=f"w_codes{w}{a}", align_bytes=64) for a in range(PASSES)] for w in range(2)]
+        w_sc = [[keep.tile([P, H], U8, name=f"w_sc{w}{a}", align_bytes=64) for a in range(PASSES)] for w in range(2)]
 
-        def quantise_weight(wi, a):
-            grouped = ring.tile([P, PACK, P, PACK], BF16, name="grouped", tag="bf", bufs=5, align_bytes=64)
-            for raw, (pw, pa, c0, cn) in zip(raws, pieces):
-                if (pw, pa) == (wi, a):
+        def quantise_weight(weight, a):
+            grouped = ring.tile([P, PACK, P, PACK], BF16, name="grouped", tag="bf16", bufs=BF16_SLOTS, align_bytes=64)
+            for raw, (piece_weight, piece_pass, c0, width) in zip(raws, pieces):
+                if (piece_weight, piece_pass) == (weight, a):
                     nc.vector.tensor_copy(
-                        out=grouped[:, :, c0 // PACK : (c0 + cn) // PACK, :].rearrange("p t m i -> p m i t"),
+                        out=grouped[:, :, c0 // PACK : (c0 + width) // PACK, :].rearrange("p t m i -> p m i t"),
                         in_=raw[:].rearrange("p i (m t) -> p m i t", t=PACK),
                     )
             nc.vector.quantize_mx(
-                out=w_codes[wi][a][:].bitcast(FP8X4), scales=w_sc[wi][a][:],
+                out=w_codes[weight][a][:].bitcast(FP8X4), scales=w_sc[weight][a][:],
                 in_=grouped[:].rearrange("p t m i -> p (t m i)"),
             )
 
-        def product(jb, which):
-            acc = psum.tile([P, BANK], F32, name="acc", tag="acc", bufs=6)
-            cols = slice(jb * P, (jb + 1) * P)
+        def product(block, moving):
+            acc = psum.tile([P, BANK], F32, name="acc", tag="acc", bufs=SUM_BANKS)
+            cols = slice(block * P, (block + 1) * P)
             for a in range(PASSES):
-                if which == 2:
-                    rhs, rhs_sc = w3_w[:, a, :].bitcast(FP4X4), w3_sc[:, a, :]
-                else:
-                    rhs, rhs_sc = w_codes[which][a][:].bitcast(FP8X4), w_sc[which][a][:]
+                codes, scales = moving(a)
                 nc.tensor.matmul_mx(
-                    out=acc[:], lhsT=v_w[a][:, cols].bitcast(FP8X4), lhsT_scale=(v_sc, v_sc1)[a][:, cols],
-                    rhs=rhs, rhs_scale=rhs_sc, start=(a == 0), stop=(a == PASSES - 1),
+                    out=acc[:], lhsT=v_w[a][:, cols].bitcast(FP8X4), lhsT_scale=v_sc[a][:, cols],
+                    rhs=codes, rhs_scale=scales, start=(a == 0), stop=(a == PASSES - 1),
                 )
-            return acc
+            return acc[:]
 
-        neg_c = [ring.tile([P, 4, PACK, P], F32, name="neg_c", tag="cf", bufs=2) for half in range(2)]
-        top = [keep.tile([P, PACK, P], F32, name=f"top{jb}") for jb in range(JB)]
-        h0 = keep.tile([P, S], F32, name="h0")
-        h2 = keep.tile([P, S], F32, name="h2")
-        y01 = keep.tile([P, 2, S], F32, name="y01")
-        y23 = keep.tile([P, 2, S], F32, name="y23")
-        h = [h0[:], y01[:, 0, :], h2[:], y23[:, 0, :]]
-        picked = [y01[:, 0, :], y01[:, 1, :], y23[:, 0, :], y23[:, 1, :]]
+        def w1_pass(a):
+            return w_codes[0][a][:].bitcast(FP8X4), w_sc[0][a][:]
 
-        def dealt(ap):
+        def w2_pass(a):
+            return w_codes[1][a][:].bitcast(FP8X4), w_sc[1][a][:]
+
+        def w3_pass(a):
+            return w3_w[:, a, :].bitcast(FP4X4), w3_sc[:, a, :]
+
+        def by_slice(ap):
             return ap.rearrange("p (t m) -> p t m", t=PACK)
 
-        larger = [top[0][:], top[1][:], top[2][:], top[3][:], dealt(wg[0][:, :BANK]), dealt(h0[:, :BANK]), top[4][:], top[5][:]]
+        neg_c = [ring.tile([P, BLOCKS // 2, PACK, P], F32, name="neg_c", tag="stage", bufs=2) for half in range(2)]
+        first_sum = [keep.tile([P, PACK, P], F32, name=f"first_sum{block}") for block in range(BLOCKS)]
+        h0 = keep.tile([P, S], F32, name="h0")
+        h2 = keep.tile([P, S], F32, name="h2")
+        picked01 = keep.tile([P, 2, M], F32, name="picked01")
+        picked23 = keep.tile([P, 2, M], F32, name="picked23")
+        h = [h0[:], picked01[:, 0, :], h2[:], picked23[:, 0, :]]
+        picked = [picked01[:, 0, :], picked01[:, 1, :], picked23[:, 0, :], picked23[:, 1, :]]
+        larger = [first_sum[block][:] for block in range(BLOCKS // 2)]
+        larger.extend([by_slice(factors[0][:, :H]), by_slice(h0[:, :H]), first_sum[4][:], first_sum[5][:]])
 
         def turn(t, blocks, dst):
-            bank = psum.tile([P, 4, P], F32, name="ht", tag="ht", bufs=2)
+            bank = psum.tile([P, BANK // P, P], F32, name="bank", tag="turn", bufs=TURN_BANKS)
             for i in reversed(range(len(blocks))):
-                jb = blocks[i]
-                o = bank[:, i, :]
-                nc.tensor.matmul(o, larger[jb][:, t, :], ident[:], start=True, stop=False, is_transpose=True)
-                nc.tensor.matmul(o, neg_c[jb // 4][:, jb % 4, t, :], ident[:], start=False, stop=True, is_transpose=True)
+                half, place = divmod(blocks[i], BLOCKS // 2)
+                nc.tensor.matmul(bank[:, i, :], larger[blocks[i]][:, t, :], ident[:], start=True, stop=False, is_transpose=True)
+                nc.tensor.matmul(bank[:, i, :], neg_c[half][:, place, t, :], ident[:], start=False, stop=True, is_transpose=True)
             nc.scalar.activation(dst, bank[:, : len(blocks), :], ACT.Copy, scale=gain_sb[:, t : t + 1])
 
         for half in range(2):
-            blocks = range(4 * half, 4 * half + 4)
-            for jb in blocks:
+            blocks = range(half * BLOCKS // 2, (half + 1) * BLOCKS // 2)
+            for place, block in enumerate(blocks):
                 nc.scalar.activation(
-                    neg_c[half][:, jb % 4, :, :].rearrange("p t m -> p m t"),
-                    product(jb, 2)[:].rearrange("p (m t) -> p m t", t=PACK), ACT.Copy, scale=-1.0,
+                    neg_c[half][:, place, :, :].rearrange("p t m -> p m t"),
+                    product(block, w3_pass).rearrange("p (m t) -> p m t", t=PACK), ACT.Copy, scale=-1.0,
                 )
             if half == 0:
                 quantise_weight(0, 0)
                 quantise_weight(0, 1)
-            for jb in blocks:
-                nc.scalar.copy(top[jb][:], dealt(product(jb, 0)[:]))
+            for block in blocks:
+                nc.scalar.copy(first_sum[block][:], by_slice(product(block, w1_pass)))
             if half == 0:
                 quantise_weight(1, 0)
                 quantise_weight(1, 1)
-            for jb in blocks:
-                nc.vector.tensor_tensor(larger[jb], top[jb][:], dealt(product(jb, 1)[:]), ALU.max)
-            for jb0 in (4 * half, 4 * half + 2):
-                cols = slice(jb0 * P, (jb0 + 2) * P)
-                turn(0, [jb0, jb0 + 1], h[0][:, cols].rearrange("p (i c) -> p i c", c=P))
+            for block in blocks:
+                nc.vector.tensor_tensor(larger[block], first_sum[block][:], by_slice(product(block, w2_pass)), ALU.max)
+            for block in (blocks[0], blocks[2]):
+                cols = slice(block * P, (block + 2) * P)
+                turn(0, [block, block + 1], h[0][:, cols].rearrange("p (i c) -> p i c", c=P))
                 nc.vector.tensor_tensor(
-                    page[0][:].indirect(idx2[:, jb0 * 8 : (jb0 + 2) * 8]), h[0][:, cols], wg[0][:, cols], ALU.mult
+                    page[0][:].indirect(entries(idx2, block * P, 2 * P)), h[0][:, cols], factors[0][:, cols], ALU.mult
                 )
         for t in range(1, PACK):
-            for e in range(2):
-                turn(t, list(range(e, JB, 2)), h[t].rearrange("p (i e c) -> p e i c", e=2, c=P)[:, e, :, :])
+            for parity in range(2):
+                dst = h[t].rearrange("p (i e c) -> p e i c", e=2, c=P)[:, parity, :, :]
+                turn(t, list(range(parity, BLOCKS, 2)), dst)
 
         mnt_sb = []
         for n in range(N // P):
-            mt = ring.tile([P, M], F32, name="mnt_sb", tag="raw", bufs=3)
-            nc.sync.dma_start(mt[:], mnt[n * P : (n + 1) * P, :])
-            mnt_sb.append(mt)
+            rows = ring.tile([P, M], F32, name="mnt_rows", tag="raw", bufs=3)
+            nc.sync.dma_start(rows[:], mnt[n * P : (n + 1) * P, :])
+            mnt_sb.append(rows)
 
-        pairs = [ring.tile([P, 2, T2 // 2], U32, name="pairs", tag="cf", bufs=2) for half in range(2)]
-        x_bf = [ring.tile([P, BANK, PACK], BF16, name="x_bf", tag="bf", bufs=5, align_bytes=64) for c in range(2)]
+        pairs = [ring.tile([P, 2, T2 // 2], U32, name="pairs", tag="stage", bufs=2) for half in range(2)]
+        x_bf = [ring.tile([P, M // 2, PACK], BF16, name="x_bf", tag="bf16", bufs=BF16_SLOTS, align_bytes=64) for half in range(2)]
 
         def scatter(t):
-            if t > 0:
-                nc.vector.tensor_tensor(page[t][:].indirect(idx2[:]), h[t], wg[t], ALU.mult)
-            nc.sync.dma_start(out1_t[t], page[t][:])
+            nc.vector.tensor_tensor(page[t][:].indirect(idx2[:]), h[t], factors[t], ALU.mult)
+
+        def store_page(t):
+            nc.sync.dma_start(out1_slices[t], page[t][:])
+
+        def gather(t, first, count):
+            nc.vector.tensor_copy(picked[t][:, first : first + count], page[t][:].indirect(entries(idx3, first, count)))
 
         def round_page(t, half):
             dst = pairs[half][:, t // 2, :].bitcast(BF16).rearrange("p (m e) -> p m e", e=2)
             nc.scalar.copy(dst[:, :, t % 2], page[t][:, half * (T2 // 2) : (half + 1) * (T2 // 2)])
 
-        def gather(t):
-            nc.vector.tensor_copy(picked[t], page[t][:].indirect(idx3[:]))
-
-        def gather_half(t, half):
-            nc.vector.tensor_copy(
-                picked[t][:, half * BANK : (half + 1) * BANK],
-                page[t][:].indirect(idx3[:, half * 32 : (half + 1) * 32]),
-            )
-
         def absolute(u, half):
-            src = (y01, y23)[u][:, :, half * BANK : (half + 1) * BANK]
+            src = (picked01, picked23)[u][:, :, half * (M // 2) : (half + 1) * (M // 2)]
             nc.scalar.activation(x_bf[half][:, :, 2 * u : 2 * u + 2], src.rearrange("p e m -> p m e"), ACT.Abs)
 
-        scatter(0)
+        store_page(0)
         scatter(1)
-        gather(0)
-        gather(1)
-        scatter(2)
-        scatter(3)
-        for half in range(2):
-            gather_half(2, half)
-            gather_half(3, half)
-        for t in range(3):
-            for half in range(2):
-                round_page(t, half)
+        store_page(1)
+        gather(0, 0, M)
+        gather(1, 0, M)
+        for t in (2, 3):
+            scatter(t)
+            store_page(t)
+        for first in (0, M // 2):
+            gather(2, first, M // 2)
+            gather(3, first, M // 2)
+        for t in range(PACK - 1):
+            round_page(t, 0)
+            round_page(t, 1)
             if t == 1:
                 absolute(0, 0)
                 absolute(0, 1)
 
         p_codes = keep.tile([P, T2], U32, name="p_codes", align_bytes=64)
         p_sc = keep.tile([P, T2], U8, name="p_sc", align_bytes=64)
-        out2_w = out_2[0].rearrange("p m i -> p (m i)").bitcast(I32)
+        out2_words = out_2[0].rearrange("p m i -> p (m i)").bitcast(I32)
 
-        def planes(c):
-            cols = slice(c * BANK, (c + 1) * BANK)
-            rounded = ring.tile([P, BANK, 2], U32, name="rounded", tag="bf", bufs=5, align_bytes=64)
-            src = pairs[c // 2][:, :, (c % 2) * BANK : (c % 2 + 1) * BANK]
-            nc.scalar.copy(rounded[:], src.rearrange("p u m -> p m u"))
+        def planes(chunk, move, word):
+            cols = slice(chunk * BANK, (chunk + 1) * BANK)
+            half, part = divmod(chunk, CHUNKS // 2)
+            joined = ring.tile([P, BANK, 2], U32, name="joined", tag="bf16", bufs=BF16_SLOTS, align_bytes=64)
+            src = pairs[half][:, :, part * BANK : (part + 1) * BANK].bitcast(word)
+            move(joined[:].bitcast(word), src.rearrange("p u m -> p m u"))
             nc.vector.quantize_mx(
                 out=p_codes[:, cols].bitcast(FP8X4), scales=p_sc[:, cols],
-                in_=rounded[:].rearrange("p m u -> p (m u)").bitcast(BF16),
+                in_=joined[:].rearrange("p m u -> p (m u)").bitcast(BF16),
             )
-            nc.sync.dma_start(out2_w[:, cols], p_codes[:, cols].bitcast(I32))
-
-        def plane_scales(half):
-            cols = slice(half * (T2 // 2), (half + 1) * (T2 // 2))
-            for q in range(4):
-                nc.sync.dma_start(
-                    out_3[0, 4 * q : 4 * q + 4, cols].bitcast(I32), p_sc[32 * q : 32 * q + 4, cols].bitcast(I32)
-                )
+            nc.sync.dma_start(out2_words[:, cols], p_codes[:, cols].bitcast(I32))
 
         def second_stage(half):
-            cols = slice(half * BANK, (half + 1) * BANK)
+            cols = slice(half * (M // 2), (half + 1) * (M // 2))
             absolute(1, half)
-            x_codes = keep.tile([P, BANK], U32, name=f"x_codes{half}", align_bytes=64)
-            x_sc = keep.tile([P, BANK], U8, name=f"x_sc{half}", align_bytes=64)
+            x_codes = keep.tile([P, M // 2], U32, name=f"x_codes{half}", align_bytes=64)
+            x_sc = keep.tile([P, M // 2], U8, name=f"x_sc{half}", align_bytes=64)
             nc.vector.quantize_mx(
                 out=x_codes[:].bitcast(FP8X4), scales=x_sc[:], in_=x_bf[half][:].rearrange("p m t -> p (m t)")
             )
             for n in range(N // P):
-                acc = psum.tile([P, BANK], F32, name="acc", tag="acc", bufs=6)
+                rows = slice(n * P, (n + 1) * P)
+                acc = psum.tile([P, BANK], F32, name="acc", tag="acc", bufs=SUM_BANKS)
                 nc.tensor.matmul_mx(
-                    out=acc[:], lhsT=w4_w[:, n * P : (n + 1) * P].bitcast(FP8X4), lhsT_scale=w4_sc[:, n * P : (n + 1) * P],
+                    out=acc[:], lhsT=w4_w[:, rows].bitcast(FP8X4), lhsT_scale=w4_sc[:, rows],
                     rhs=x_codes[:].bitcast(FP8X4), rhs_scale=x_sc[:], start=True, stop=True,
                 )
                 nc.vector.tensor_tensor(mnt_sb[n][:, cols], acc[:], mnt_sb[n][:, cols], ALU.add)
-                nc.sync.dma_start(out_0[n * P : (n + 1) * P, cols], mnt_sb[n][:, cols])
+                nc.sync.dma_start(out_0[rows, cols], mnt_sb[n][:, cols])
 
-        round_page(3, 0)
+        round_page(PACK - 1, 0)
+        round_page(PACK - 1, 1)
         second_stage(0)
-        planes(0)
+        planes(0, nc.vector.tensor_copy, I32)
         second_stage(1)
-        planes(1)
-        plane_scales(0)
-        round_page(3, 1)
-        planes(2)
-        planes(3)
-        plane_scales(1)
+        for chunk in range(1, CHUNKS):
+            planes(chunk, nc.scalar.copy, U32)
+        for q in range(QUADRANTS):
+            nc.sync.dma_start(out_3[0, 4 * q : 4 * q + 4, :].bitcast(I32), live_rows(p_sc, q))

from contextlib import ExitStack

import concourse.mybir as mybir
from concourse.masks import make_identity

K, T, S, H, N, T2, M = 1024, 4096, 1024, 512, 384, 2048, 1024
FLOPS = 3 * 2 * K * H * S + 2 * H * N * M

F32 = mybir.dt.float32
BF16 = mybir.dt.bfloat16
I32 = mybir.dt.int32
U32 = mybir.dt.uint32
U16 = mybir.dt.uint16
U8 = mybir.dt.uint8
FP8X4 = mybir.dt.float8_e4m3fn_x4
FP4X4 = mybir.dt.float4_e2m1fn_x4
ACT = mybir.ActivationFunctionType
ALU = mybir.AluOpType

P = 128
PACK = 4
K_PASS = P * PACK
PASSES = K // K_PASS
BANK = 512
QUADRANTS = 4
GROUP = 16
BLOCKS = S // P
CHUNKS = T2 // BANK
SPARE_ROWS = 8
SUM_BANKS = 6
TURN_BANKS = 2
BF16_SLOTS = 5


def tile_list_chord_span_archive_kernel(
    tc, tab_words, tab_scales, offs, w1, w2, w3_words, w3_scales, gain, wgs, page0,
    offs2, offs3, w4_words, w4_scales, mnt, out_0, out_1, out_2, out_3,
):
    nc = tc.nc
    with ExitStack() as ctx:
        lists = ctx.enter_context(tc.tile_pool(name="lists", bufs=1))
        keep = ctx.enter_context(tc.tile_pool(name="keep", bufs=1))
        ring = ctx.enter_context(tc.tile_pool(name="ring", bufs=1))
        psum = ctx.enter_context(tc.psum_pool(name="psum", bufs=1))

        idx1 = lists.tile([P, S // GROUP], U16, name="idx1")
        idx2 = lists.tile([P, S // GROUP], U16, name="idx2")
        idx3 = lists.tile([P, M // GROUP], U16, name="idx3")

        def entries(idx, first, count):
            return idx[:, first // GROUP : (first + count) // GROUP]

        def live_rows(tile, q):
            return tile[32 * q : 32 * q + 4].bitcast(I32)

        tab_sc = keep.tile([P, T], U8, name="tab_sc", align_bytes=64)
        v_sc1 = keep.tile([P, S], U8, name="v_sc1", align_bytes=64)
        w3_sc = keep.tile([P, PASSES, H], U8, name="w3_sc", align_bytes=64)
        w4_sc = keep.tile([P, N], U8, name="w4_sc", align_bytes=64)
        nc.vector.memset(tab_sc[:, : T // 2].bitcast(I32), 0)
        nc.gpsimd.memset(tab_sc[:, T // 2 :].bitcast(I32), 0)
        nc.vector.memset(w3_sc[:].bitcast(I32), 0)
        nc.vector.memset(v_sc1[:].bitcast(I32), 0)
        nc.vector.memset(w4_sc[:].bitcast(I32), 0)

        nc.sync.dma_start(idx1[:], offs)
        tab_w = [keep.tile([P, T], U32, name=f"tab_w{a}") for a in range(PASSES)]
        tab_src = [tab_words[a].rearrange("p t i -> p (t i)").bitcast(I32) for a in range(PASSES)]
        nc.sync.dma_start(tab_w[0][:, : T // 2].bitcast(I32), tab_src[0][:, : T // 2])
        nc.sync.dma_start(idx2[:], offs2)
        for q in range(QUADRANTS):
            nc.sync.dma_start(live_rows(tab_sc, q), tab_scales[0, 4 * q : 4 * q + 4, :].bitcast(I32))
        nc.sync.dma_start(tab_sc[SPARE_ROWS : SPARE_ROWS + 16, :].bitcast(I32), tab_scales[1].bitcast(I32))
        nc.sync.dma_start(tab_w[0][:, T // 2 :].bitcast(I32), tab_src[0][:, T // 2 :])
        w3_w = keep.tile([P, PASSES, 2 * H], U8, name="w3_w", align_bytes=64)
        nc.sync.dma_start(w3_w[:].bitcast(I32), w3_words.rearrange("a p c -> p a c").bitcast(I32))
        for q in range(QUADRANTS):
            nc.sync.dma_start(
                live_rows(w3_sc, q), w3_scales[:, 4 * q : 4 * q + 4, :].rearrange("a s c -> s a c").bitcast(I32)
            )
        nc.sync.dma_start(tab_w[1][:].bitcast(I32), tab_src[1])
        v_sc0 = keep.tile([P, S], U8, name="v_sc0", align_bytes=64)
        nc.vector.tensor_copy(v_sc0[:], tab_sc[:].indirect(idx1[:]))
        for q in range(QUADRANTS):
            first = SPARE_ROWS + 4 * q
            nc.sync.dma_start(live_rows(v_sc1, q), v_sc0[first : first + 4, :].bitcast(I32))
        v_sc = (v_sc0, v_sc1)

        pieces = [(0, 0, 0, H), (0, 1, 0, H), (1, 0, 0, H), (1, 1, 0, H // 2), (1, 1, H // 2, H // 2)]
        raws = []
        for weight, a, c0, width in pieces:
            whole = width == H
            raw = ring.tile([P, PACK, width], F32, name="raw", tag="raw" if whole else "raw_half", bufs=3 if whole else 2)
            rows = (w1, w2)[weight][a * K_PASS : (a + 1) * K_PASS, c0 : c0 + width]
            nc.sync.dma_start(raw[:], rows.rearrange("(p i) c -> p i c", i=PACK))
            raws.append(raw)

        gain_sb = keep.tile([P, PACK], F32, name="gain_sb")
        nc.sync.dma_start(gain_sb[:], gain.rearrange("(p t) -> p t", t=PACK))
        nc.sync.dma_start(idx3[:], offs3)
        page0_slices = page0.rearrange("(p t) m -> t p m", t=PACK)
        out1_slices = out_1.rearrange("(p t) m -> t p m", t=PACK)
        wgs_rows = wgs.rearrange("(u t) j -> u t j", t=PACK)

        def load_page(t):
            tile = keep.tile([P, T2], F32, name=f"page{t}")
            nc.sync.dma_start(tile[:], page0_slices[t])
            return tile

        def load_factors(t, count, column_ranges):
            tile = keep.tile([P, count, S], F32, name=f"factors{t}")
            for cols in column_ranges:
                for q in (0, 2, 1, 3):
                    nc.sync.dma_start(tile[32 * q : 32 * q + 32, :, cols], wgs_rows[:, t : t + count, cols])
            return [tile[:, i, :] for i in range(count)]

        page = [load_page(0)]
        factors = load_factors(0, 1, [slice(0, S // 2), slice(S // 2, S)])
        factors.extend(load_factors(1, 1, [slice(0, S)]))
        page.append(load_page(1))
        factors.extend(load_factors(2, 2, [slice(0, S)]))
        page.append(load_page(2))
        page.append(load_page(3))
        w4_w = keep.tile([P, N], U32, name="w4_w", align_bytes=64)
        nc.sync.dma_start(w4_w[:].bitcast(I32), w4_words[0].rearrange("p c i -> p (c i)").bitcast(I32))
        for q in range(QUADRANTS):
            nc.sync.dma_start(live_rows(w4_sc, q), w4_scales[0, 4 * q : 4 * q + 4, :].bitcast(I32))

        ident = keep.tile([P, P], F32, name="ident")
        make_identity(nc, ident[:])

        v_w = [keep.tile([P, S], U32, name=f"v_w{a}", align_bytes=64) for a in range(PASSES)]
        nc.vector.tensor_copy(v_w[0][:], tab_w[0][:].indirect(idx1[:]))
        for first in (0, S // 2):
            nc.vector.tensor_copy(v_w[1][:, first : first + S // 2], tab_w[1][:].indirect(entries(idx1, first, S // 2)))

        w_codes = [[keep.tile([P, H], U32, name=f"w_codes{w}{a}", align_bytes=64) for a in range(PASSES)] for w in range(2)]
        w_sc = [[keep.tile([P, H], U8, name=f"w_sc{w}{a}", align_bytes=64) for a in range(PASSES)] for w in range(2)]

        def quantise_weight(weight, a):
            grouped = ring.tile([P, PACK, P, PACK], BF16, name="grouped", tag="bf16", bufs=BF16_SLOTS, align_bytes=64)
            for raw, (piece_weight, piece_pass, c0, width) in zip(raws, pieces):
                if (piece_weight, piece_pass) == (weight, a):
                    nc.vector.tensor_copy(
                        out=grouped[:, :, c0 // PACK : (c0 + width) // PACK, :].rearrange("p t m i -> p m i t"),
                        in_=raw[:].rearrange("p i (m t) -> p m i t", t=PACK),
                    )
            nc.vector.quantize_mx(
                out=w_codes[weight][a][:].bitcast(FP8X4), scales=w_sc[weight][a][:],
                in_=grouped[:].rearrange("p t m i -> p (t m i)"),
            )

        def product(block, moving):
            acc = psum.tile([P, BANK], F32, name="acc", tag="acc", bufs=SUM_BANKS)
            cols = slice(block * P, (block + 1) * P)
            for a in range(PASSES):
                codes, scales = moving(a)
                nc.tensor.matmul_mx(
                    out=acc[:], lhsT=v_w[a][:, cols].bitcast(FP8X4), lhsT_scale=v_sc[a][:, cols],
                    rhs=codes, rhs_scale=scales, start=(a == 0), stop=(a == PASSES - 1),
                )
            return acc[:]

        def w1_pass(a):
            return w_codes[0][a][:].bitcast(FP8X4), w_sc[0][a][:]

        def w2_pass(a):
            return w_codes[1][a][:].bitcast(FP8X4), w_sc[1][a][:]

        def w3_pass(a):
            return w3_w[:, a, :].bitcast(FP4X4), w3_sc[:, a, :]

        def by_slice(ap):
            return ap.rearrange("p (t m) -> p t m", t=PACK)

        neg_c = [ring.tile([P, BLOCKS // 2, PACK, P], F32, name="neg_c", tag="stage", bufs=2) for half in range(2)]
        first_sum = [keep.tile([P, PACK, P], F32, name=f"first_sum{block}") for block in range(BLOCKS)]
        h0 = keep.tile([P, S], F32, name="h0")
        h2 = keep.tile([P, S], F32, name="h2")
        picked01 = keep.tile([P, 2, M], F32, name="picked01")
        picked23 = keep.tile([P, 2, M], F32, name="picked23")
        h = [h0[:], picked01[:, 0, :], h2[:], picked23[:, 0, :]]
        picked = [picked01[:, 0, :], picked01[:, 1, :], picked23[:, 0, :], picked23[:, 1, :]]
        larger = [first_sum[block][:] for block in range(BLOCKS // 2)]
        larger.extend([by_slice(factors[0][:, :H]), by_slice(h0[:, :H]), first_sum[4][:], first_sum[5][:]])

        def turn(t, blocks, dst):
            bank = psum.tile([P, BANK // P, P], F32, name="bank", tag="turn", bufs=TURN_BANKS)
            for i in reversed(range(len(blocks))):
                half, place = divmod(blocks[i], BLOCKS // 2)
                nc.tensor.matmul(bank[:, i, :], larger[blocks[i]][:, t, :], ident[:], start=True, stop=False, is_transpose=True)
                nc.tensor.matmul(bank[:, i, :], neg_c[half][:, place, t, :], ident[:], start=False, stop=True, is_transpose=True)
            nc.scalar.activation(dst, bank[:, : len(blocks), :], ACT.Copy, scale=gain_sb[:, t : t + 1])

        for half in range(2):
            blocks = range(half * BLOCKS // 2, (half + 1) * BLOCKS // 2)
            for place, block in enumerate(blocks):
                nc.scalar.activation(
                    neg_c[half][:, place, :, :].rearrange("p t m -> p m t"),
                    product(block, w3_pass).rearrange("p (m t) -> p m t", t=PACK), ACT.Copy, scale=-1.0,
                )
            if half == 0:
                quantise_weight(0, 0)
                quantise_weight(0, 1)
            for block in blocks:
                nc.scalar.copy(first_sum[block][:], by_slice(product(block, w1_pass)))
            if half == 0:
                quantise_weight(1, 0)
                quantise_weight(1, 1)
            for block in blocks:
                nc.vector.tensor_tensor(larger[block], first_sum[block][:], by_slice(product(block, w2_pass)), ALU.max)
            for block in (blocks[0], blocks[2]):
                cols = slice(block * P, (block + 2) * P)
                turn(0, [block, block + 1], h[0][:, cols].rearrange("p (i c) -> p i c", c=P))
                nc.vector.tensor_tensor(
                    page[0][:].indirect(entries(idx2, block * P, 2 * P)), h[0][:, cols], factors[0][:, cols], ALU.mult
                )
        for t in range(1, PACK):
            for parity in range(2):
                dst = h[t].rearrange("p (i e c) -> p e i c", e=2, c=P)[:, parity, :, :]
                turn(t, list(range(parity, BLOCKS, 2)), dst)

        mnt_sb = []
        for n in range(N // P):
            rows = ring.tile([P, M], F32, name="mnt_rows", tag="raw", bufs=3)
            nc.sync.dma_start(rows[:], mnt[n * P : (n + 1) * P, :])
            mnt_sb.append(rows)

        pairs = [ring.tile([P, 2, T2 // 2], U32, name="pairs", tag="stage", bufs=2) for half in range(2)]
        x_bf = [ring.tile([P, M // 2, PACK], BF16, name="x_bf", tag="bf16", bufs=BF16_SLOTS, align_bytes=64) for half in range(2)]

        def scatter(t):
            nc.vector.tensor_tensor(page[t][:].indirect(idx2[:]), h[t], factors[t], ALU.mult)

        def store_page(t):
            nc.sync.dma_start(out1_slices[t], page[t][:])

        def gather(t, first, count):
            nc.vector.tensor_copy(picked[t][:, first : first + count], page[t][:].indirect(entries(idx3, first, count)))

        def round_page(t, half):
            dst = pairs[half][:, t // 2, :].bitcast(BF16).rearrange("p (m e) -> p m e", e=2)
            nc.scalar.copy(dst[:, :, t % 2], page[t][:, half * (T2 // 2) : (half + 1) * (T2 // 2)])

        def absolute(u, half):
            src = (picked01, picked23)[u][:, :, half * (M // 2) : (half + 1) * (M // 2)]
            nc.scalar.activation(x_bf[half][:, :, 2 * u : 2 * u + 2], src.rearrange("p e m -> p m e"), ACT.Abs)

        store_page(0)
        scatter(1)
        store_page(1)
        gather(0, 0, M)
        gather(1, 0, M)
        for t in (2, 3):
            scatter(t)
            store_page(t)
        for first in (0, M // 2):
            gather(2, first, M // 2)
            gather(3, first, M // 2)
        for t in range(PACK - 1):
            round_page(t, 0)
            round_page(t, 1)
            if t == 1:
                absolute(0, 0)
                absolute(0, 1)

        p_codes = keep.tile([P, T2], U32, name="p_codes", align_bytes=64)
        p_sc = keep.tile([P, T2], U8, name="p_sc", align_bytes=64)
        out2_words = out_2[0].rearrange("p m i -> p (m i)").bitcast(I32)

        def planes(chunk, move, word):
            cols = slice(chunk * BANK, (chunk + 1) * BANK)
            half, part = divmod(chunk, CHUNKS // 2)
            joined = ring.tile([P, BANK, 2], U32, name="joined", tag="bf16", bufs=BF16_SLOTS, align_bytes=64)
            src = pairs[half][:, :, part * BANK : (part + 1) * BANK].bitcast(word)
            move(joined[:].bitcast(word), src.rearrange("p u m -> p m u"))
            nc.vector.quantize_mx(
                out=p_codes[:, cols].bitcast(FP8X4), scales=p_sc[:, cols],
                in_=joined[:].rearrange("p m u -> p (m u)").bitcast(BF16),
            )
            nc.sync.dma_start(out2_words[:, cols], p_codes[:, cols].bitcast(I32))

        def second_stage(half):
            cols = slice(half * (M // 2), (half + 1) * (M // 2))
            absolute(1, half)
            x_codes = keep.tile([P, M // 2], U32, name=f"x_codes{half}", align_bytes=64)
            x_sc = keep.tile([P, M // 2], U8, name=f"x_sc{half}", align_bytes=64)
            nc.vector.quantize_mx(
                out=x_codes[:].bitcast(FP8X4), scales=x_sc[:], in_=x_bf[half][:].rearrange("p m t -> p (m t)")
            )
            for n in range(N // P):
                rows = slice(n * P, (n + 1) * P)
                acc = psum.tile([P, BANK], F32, name="acc", tag="acc", bufs=SUM_BANKS)
                nc.tensor.matmul_mx(
                    out=acc[:], lhsT=w4_w[:, rows].bitcast(FP8X4), lhsT_scale=w4_sc[:, rows],
                    rhs=x_codes[:].bitcast(FP8X4), rhs_scale=x_sc[:], start=True, stop=True,
                )
                nc.vector.tensor_tensor(mnt_sb[n][:, cols], acc[:], mnt_sb[n][:, cols], ALU.add)
                nc.sync.dma_start(out_0[rows, cols], mnt_sb[n][:, cols])

        round_page(PACK - 1, 0)
        round_page(PACK - 1, 1)
        second_stage(0)
        planes(0, nc.vector.tensor_copy, I32)
        second_stage(1)
        for chunk in range(1, CHUNKS):
            planes(chunk, nc.scalar.copy, U32)
        for q in range(QUADRANTS):
            nc.sync.dma_start(out_3[0, 4 * q : 4 * q + 4, :].bitcast(I32), live_rows(p_sc, q))
